import numpy as np
import ml_dtypes


def mxq(x, axis, fmt="e4m3"):
    dtype, down = {"e4m3": (ml_dtypes.float8_e4m3fn, 7), "e5m2": (ml_dtypes.float8_e5m2, 14)}[fmt]
    v = np.moveaxis(np.asarray(x, np.float32).astype(ml_dtypes.bfloat16).astype(np.float64), axis, -1)
    blocks = v.reshape(v.shape[:-1] + (-1, 32))
    amax = np.abs(blocks).max(-1, keepdims=True)
    byte = np.maximum(np.where(amax > 0, np.frexp(amax)[1] - 1 + 127, 0) - down, 1)
    scale = np.exp2(byte - 127.0)
    codes = (blocks / scale).astype(np.float32).astype(dtype).astype(np.float64)
    return np.moveaxis((codes * scale).reshape(v.shape), -1, axis)


WIDE = False


def mx_kscale(k):
    if not WIDE:
        return np.ones(k)
    levels = np.array([10, -10, 5, -5, 0])
    if k % 512:
        return np.exp2(np.random.permutation(np.resize(levels, k // 32))).repeat(32)
    a = np.empty((k // 512, 16))
    for p in range(k // 512):
        a[p, :8] = np.random.permutation(np.resize(levels, 8))
        for g in range(8):
            far = levels[np.abs(levels - a[p, g]) >= 10]
            a[p, g + 8] = far[np.random.randint(len(far))]
    return np.exp2(a.ravel()).repeat(32)


def f64(x):
    return np.asarray(x).astype(np.float64)


def striped(idx):
    return np.tile(idx.reshape(-1, 16).T, (8, 1)).astype(np.uint16)


def unstriped(offs):
    return offs[:16].T.reshape(-1).astype(np.int64)


def striped8(idx):
    return np.concatenate([x.reshape(-1, 16).T for x in idx]).astype(np.uint16)


def runs(offs, k):
    lists = np.stack([offs[16 * r : 16 * r + 16].T.reshape(-1) for r in range(8)]).astype(np.int64)
    return lists[np.arange(k) % 512 // 64]


def pack_weight(w):
    k, n = w.shape
    w = f64(np.asarray(w, np.float32).astype(ml_dtypes.bfloat16)).reshape(k // 32, 32, n)
    amax = np.abs(w).max(1)
    byte = np.clip(np.where(amax > 0, np.frexp(amax)[1] - 1 + 127 - 7, 1), 1, 254)
    scaled = (w * np.exp2(127.0 - byte)[:, None, :]).reshape(k, n).astype(np.float32)
    words = np.ascontiguousarray(scaled.reshape(k // 512, 128, 4, n).transpose(0, 1, 3, 2)).astype(ml_dtypes.float8_e4m3fn).view(np.uint8)
    return words, np.ascontiguousarray(byte.astype(np.uint8).reshape(k // 512, 16, n))


def unpack_weight(words, scales):
    g, p, n, _ = words.shape
    vals = np.ascontiguousarray(words).view(ml_dtypes.float8_e4m3fn).astype(np.float64) * np.repeat(np.exp2(scales.astype(np.float64) - 127.0), 8, axis=1)[..., None]
    return vals.transpose(0, 1, 3, 2).reshape(g * 512, n)


K, T, S, N, H, G = 512, 2048, 512, 512, 512, 2048


def setup_inputs():
    n = np.random.standard_normal
    s = mx_kscale(K)[:, None]
    u = mx_kscale(S)
    packed_xT = pack_weight(n((K, T)) * s)
    packed_dT = pack_weight(n((K, G)) / s)
    return {
        "x_words": packed_xT[0],
        "x_scales": packed_xT[1],
        "w1": (n((K, H)) / np.sqrt(K) / s).astype(np.float32),
        "gn": (np.random.uniform(0.5, 1.5, (H, 1)) * u[:, None]).astype(np.float32),
        "w2": (n((H, N)) / np.sqrt(H) / u[:, None]).astype(np.float32),
        "d_words": packed_dT[0],
        "d_scales": packed_dT[1],
        "offs": striped(np.random.permutation(T)[:S]),
        "n1": striped8(np.stack([np.random.permutation(S) for _ in range(8)])),
        "n2": striped8(np.stack([np.random.permutation(S) for _ in range(8)])),
        "two": striped(np.random.permutation(T)[:S]),
        "k1": striped8(np.random.randint(0, G, (8, H))),
        "n3": striped(np.random.permutation(S)),
        "n4": striped(np.random.permutation(S)),
        "n5": striped(np.random.permutation(S)),
    }


def reference(x_words, x_scales, w1, gn, w2, d_words, d_scales, offs, n1, n2, two, k1, n3, n4, n5):
    xq = unpack_weight(x_words, x_scales)[:, unstriped(offs)]
    y = mxq(f64(w1), 0, "e4m3").T @ xq
    z = f64(gn) * (np.minimum(np.maximum(y, y[np.arange(H)[:, None], runs(n1, H)]), y[np.arange(H)[:, None], runs(n2, H)]))
    a = mxq(f64(w2), 0, "e4m3").T @ mxq(z, 0, "e4m3")
    d_k1 = unpack_weight(d_words, d_scales)[np.arange(K)[:, None], runs(k1, K)]
    x_two = unpack_weight(x_words, x_scales)[:, unstriped(two)]
    b = 0.0625 * (d_k1.T @ x_two)
    return np.maximum(np.minimum(a - (0.5 * a[:, unstriped(n3)]), b[:, unstriped(n4)]), b[:, unstriped(n5)])

@@ -1,0 +1,203 @@
+from contextlib import ExitStack
+
+import concourse.mybir as mybir
+
+K, T, S, N, H, G = 512, 2048, 512, 512, 512, 2048
+FLOPS = 2 * (K * H * S + H * N * S + K * H * S)
+
+F32 = mybir.dt.float32
+BF16 = mybir.dt.bfloat16
+I32 = mybir.dt.int32
+U32 = mybir.dt.uint32
+U16 = mybir.dt.uint16
+U8 = mybir.dt.uint8
+FP8X4 = mybir.dt.float8_e4m3fn_x4
+ALU = mybir.AluOpType
+ACT = mybir.ActivationFunctionType
+
+P = 128
+PACK = 4
+TILES = 4
+Y_WINDOW = 1024
+AB_WINDOW = 704
+
+
+def tile_picked_cdjoinclampbminmx_none_p_kernel(
+    tc, x_words, x_scales, w1, gn, w2, d_words, d_scales, offs, n1, n2, two, k1, n3, n4, n5, out
+):
+    nc = tc.nc
+    with ExitStack() as ctx:
+        keep = ctx.enter_context(tc.tile_pool(name="keep", bufs=1))
+        psum = ctx.enter_context(tc.psum_pool(name="psum", bufs=1))
+
+        def sb(name, shape, dtype, tag=None):
+            return keep.tile(shape, dtype, name=name, tag=tag or name, align_bytes=64)
+
+        def load_list(name, dram):
+            tile = sb(name, [P, S // 16], U16)
+            nc.sync.dma_start(tile[:], dram)
+            return tile
+
+        def load_words(name, dram):
+            tile = sb(name, [P, T], U32)
+            nc.sync.dma_start(tile[:].bitcast(I32), dram[0].rearrange("p n t -> p (n t)").bitcast(I32))
+            return tile
+
+        def zeroed_bytes(name, width, engine):
+            tile = sb(name, [P, width], U8)
+            engine.memset(tile[:].bitcast(I32), 0)
+            return tile
+
+        def gather_v(name, window, lst, dtype):
+            tile = sb(name, [P, S], dtype)
+            nc.vector.tensor_copy(tile[:], window[:].indirect(lst[:]))
+            return tile
+
+        def gather_on(engine, dst, window, lst):
+            if engine == "vector":
+                nc.vector.tensor_copy(dst, window[:].indirect(lst[:]))
+            else:
+                nc.scalar.activation(dst, window[:].indirect(lst[:]), ACT.Copy)
+
+        def quantize(name, grouped):
+            codes = sb(name + "_codes", [P, S], U32)
+            scales = sb(name + "_scales", [P, S], U8)
+            nc.vector.quantize_mx(out=codes[:].bitcast(FP8X4), scales=scales[:], in_=grouped)
+            return codes, scales
+
+        def product(bank, lhs, rhs, t):
+            cols = slice(P * t, P * (t + 1))
+            nc.tensor.matmul_mx(
+                out=bank[:], lhsT=lhs[0][:, cols].bitcast(FP8X4), lhsT_scale=lhs[1][:, cols],
+                rhs=rhs[0][:].bitcast(FP8X4), rhs_scale=rhs[1][:], start=True, stop=True,
+            )
+
+        xs = zeroed_bytes("xs", T, nc.gpsimd)
+        ds = zeroed_bytes("ds", G, nc.vector)
+        ds_placed = zeroed_bytes("ds_placed", S, nc.vector)
+        w1_rows = w1.rearrange("(p j) c -> p j c", j=PACK)
+        w1_half = [sb(f"w1_half{h}", [P, PACK, H // 2], F32) for h in range(2)]
+
+        offs_t = load_list("offs_t", offs)
+        for q in range(4):
+            nc.sync.dma_start(xs[32 * q : 32 * q + 4, :].bitcast(I32), x_scales[0, 4 * q : 4 * q + 4, :].bitcast(I32))
+        nc.sync.dma_start(w1_half[0][:], w1_rows[:, :, : H // 2])
+        two_t = load_list("two_t", two)
+        nc.sync.dma_start(w1_half[1][:], w1_rows[:, :, H // 2 :])
+        k1_t = load_list("k1_t", k1)
+        nc.sync.dma_start(ds[0:P:8, :].bitcast(I32), d_scales[0].bitcast(I32))
+        gain = sb("gain", [P, PACK], F32)
+        nc.sync.dma_start(gain[:], gn.rearrange("(p t) o -> p (t o)", t=PACK))
+        xw = load_words("xw", x_words)
+        n1_t = load_list("n1_t", n1)
+        n2_t = load_list("n2_t", n2)
+        w2_raw = sb("w2_raw", [P, PACK, N], F32)
+        nc.sync.dma_start(w2_raw[:], w2.rearrange("(p j) c -> p j c", j=PACK))
+        dw = load_words("dw", d_words)
+        n4_t = load_list("n4_t", n4)
+        n5_t = load_list("n5_t", n5)
+        n3_t = load_list("n3_t", n3)
+
+        y_win = [sb(f"y_win{t}", [P, Y_WINDOW], F32) for t in range(TILES)]
+        a_win = [sb(f"a_win{t}", [P, AB_WINDOW], F32) for t in range(TILES)]
+        b_win = [sb(f"b_win{t}", [P, AB_WINDOW], F32) for t in range(TILES)]
+        for t in range(TILES):
+            nc.vector.memset(y_win[t][:, S:], 0.0)
+        for t in range(TILES):
+            nc.gpsimd.memset(b_win[t][:, S:], 0.0)
+            nc.gpsimd.memset(a_win[t][:, S:], 0.0)
+
+        w1_grouped = sb("w1_grouped", [P, TILES, P, PACK], BF16)
+        for h in range(2):
+            nc.scalar.copy(
+                w1_grouped[:, :, 64 * h : 64 * (h + 1), :].rearrange("p t m j -> p m j t"),
+                w1_half[h][:].rearrange("p j (m t) -> p m j t", t=TILES),
+            )
+        gain_abs = sb("gain_abs", [P, PACK], F32)
+        gain_sign = sb("gain_sign", [P, PACK], F32)
+        nc.scalar.activation(gain_abs[:], gain[:], ACT.Abs)
+        nc.scalar.activation(gain_sign[:], gain[:], ACT.Sign)
+
+        xs_offs = gather_v("xs_offs", xs, offs_t, U8)
+        w1q = quantize("w1q", w1_grouped[:].rearrange("p t m j -> p (t m j)"))
+        xw_offs = gather_v("xw_offs", xw, offs_t, U32)
+        y_bank = [psum.tile([P, S], F32, name=f"y_bank{t}", tag=f"ya{t}") for t in range(TILES)]
+        for t in range(TILES):
+            product(y_bank[t], w1q, (xw_offs, xs_offs), t)
+
+        xs_two = gather_v("xs_two", xs, two_t, U8)
+        ds_k1 = gather_v("ds_k1", ds, k1_t, U8)
+        for q in range(4):
+            nc.sync.dma_start(ds_placed[32 * q : 32 * q + 4, :].bitcast(I32), ds_k1[32 * q : 32 * q + 32 : 8, :].bitcast(I32))
+        xw_two = gather_v("xw_two", xw, two_t, U32)
+
+        w2_grouped = sb("w2_grouped", [P, N, PACK], BF16)
+        nc.gpsimd.tensor_tensor(
+            w2_grouped[:].rearrange("p (c i) j -> p c j i", i=4),
+            w2_raw[:].rearrange("p j (c i) -> p c j i", i=4),
+            gain_sign[:].unsqueeze(1).unsqueeze(3).to_broadcast([P, N // 4, PACK, 4]),
+            ALU.mult,
+        )
+
+        y_n1 = sb("y_n1", [P, TILES, S], F32)
+        y_n2 = sb("y_n2", [P, TILES, S], F32)
+        larger = sb("larger", [P, TILES, S], F32)
+        for t in range(TILES):
+            nc.scalar.activation(y_win[t][:, :S], y_bank[t][:], ACT.Copy, scale=gain_abs[:, t : t + 1])
+        for t in range(TILES):
+            gather_on("scalar", y_n1[:, t, :], y_win[t], n1_t)
+            gather_on("vector", y_n2[:, t, :], y_win[t], n2_t)
+            nc.vector.scalar_tensor_tensor(
+                larger[:, t, :], y_bank[t][:], gain_abs[:, t : t + 1], y_n1[:, t, :], ALU.mult, ALU.max
+            )
+        dw_k1 = gather_v("dw_k1", dw, k1_t, U32)
+        b_bank = [psum.tile([P, S], F32, name=f"b_bank{t}", tag=f"b{t}") for t in range(TILES)]
+        for t in range(TILES):
+            product(b_bank[t], (dw_k1, ds_placed), (xw_two, xs_two), t)
+        w2q = quantize("w2q", w2_grouped[:].rearrange("p c j -> p (c j)"))
+        z_grouped = sb("z_grouped", [P, S, PACK], BF16, tag="w2_grouped")
+        z_codes = sb("z_codes", [P, S], U32)
+        z_scales = sb("z_scales", [P, S], U8)
+        for h in range(2):
+            cols = slice(256 * h, 256 * (h + 1))
+            nc.vector.tensor_tensor(
+                z_grouped[:, cols, :].rearrange("p (c i) t -> p c t i", i=4),
+                larger[:, :, cols].rearrange("p t (c i) -> p c t i", i=4),
+                y_n2[:, :, cols].rearrange("p t (c i) -> p c t i", i=4),
+                ALU.min,
+            )
+        for h in range(2):
+            cols = slice(256 * h, 256 * (h + 1))
+            nc.vector.quantize_mx(
+                out=z_codes[:, cols].bitcast(FP8X4), scales=z_scales[:, cols],
+                in_=z_grouped[:, cols, :].rearrange("p c t -> p (c t)"),
+            )
+        a_bank = [psum.tile([P, S], F32, name=f"a_bank{t}", tag=f"ya{t}") for t in range(TILES)]
+        for t in range(TILES):
+            product(a_bank[t], w2q, (z_codes, z_scales), t)
+
+        for t in range(TILES):
+            nc.scalar.activation(b_win[t][:, :S], b_bank[t][:], ACT.Copy, scale=0.0625)
+        last = TILES - 1
+        b_n5_early = sb("b_n5_early", [P, last, S], F32, tag="larger")
+        b_n4 = [sb(f"b_n4_{t}", [P, S], F32)[:] for t in range(last)]
+        b_n5 = [b_n5_early[:, t, :] for t in range(last)]
+        for t in range(last):
+            gather_on("scalar", b_n4[t], b_win[t], n4_t)
+            gather_on("vector", b_n5[t], b_win[t], n5_t)
+        for t in range(TILES):
+            a_n3 = sb(f"a_n3_{t}", [P, S], F32)
+            nc.scalar.copy(a_win[t][:, :S], a_bank[t][:])
+            gather_on("scalar", a_n3[:], a_win[t], n3_t)
+            if t == last:
+                b_n4.append(sb("b_n4_last", [P, S], F32, tag=f"a_win{t - 1}")[:])
+                b_n5.append(sb("b_n5_last", [P, S], F32, tag=f"a_win{t}")[:])
+                gather_on("scalar", b_n4[t], b_win[t], n4_t)
+                gather_on("scalar", b_n5[t], b_win[t], n5_t)
+            diff = sb(f"diff{t}", [P, S], F32)
+            low = sb(f"low{t}", [P, S], F32)
+            res = sb(f"res{t}", [P, S], F32)
+            nc.vector.scalar_tensor_tensor(diff[:], a_n3[:], -0.5, a_bank[t][:], ALU.mult, ALU.add)
+            nc.vector.tensor_tensor(low[:], diff[:], b_n4[t], ALU.min)
+            nc.vector.tensor_tensor(res[:], low[:], b_n5[t], ALU.max)
+            nc.sync.dma_start(out[P * t : P * (t + 1), :], res[:])

@@ -72,23 +72,23 @@ def tile_picked_cdjoinclampbminmx_none_p_kernel(
                 rhs=rhs[0][:].bitcast(FP8X4), rhs_scale=rhs[1][:], start=True, stop=True,
             )
 
-        xs = zeroed_bytes("xs", T, nc.gpsimd)
+        xs = zeroed_bytes("xs", T, nc.vector)
         ds = zeroed_bytes("ds", G, nc.vector)
         ds_placed = zeroed_bytes("ds_placed", S, nc.vector)
         w1_rows = w1.rearrange("(p j) c -> p j c", j=PACK)
         w1_half = [sb(f"w1_half{h}", [P, PACK, H // 2], F32) for h in range(2)]
 
         offs_t = load_list("offs_t", offs)
+        k1_t = load_list("k1_t", k1)
+        nc.sync.dma_start(w1_half[0][:], w1_rows[:, :, : H // 2])
         for q in range(4):
             nc.sync.dma_start(xs[32 * q : 32 * q + 4, :].bitcast(I32), x_scales[0, 4 * q : 4 * q + 4, :].bitcast(I32))
-        nc.sync.dma_start(w1_half[0][:], w1_rows[:, :, : H // 2])
-        two_t = load_list("two_t", two)
         nc.sync.dma_start(w1_half[1][:], w1_rows[:, :, H // 2 :])
-        k1_t = load_list("k1_t", k1)
         nc.sync.dma_start(ds[0:P:8, :].bitcast(I32), d_scales[0].bitcast(I32))
-        gain = sb("gain", [P, PACK], F32)
-        nc.sync.dma_start(gain[:], gn.rearrange("(p t) o -> p (t o)", t=PACK))
         xw = load_words("xw", x_words)
+        two_t = load_list("two_t", two)
+        gain = sb("gain", [P, PACK], F32)
+        nc.gpsimd.dma_start(gain[:], gn.rearrange("(p t) o -> p (t o)", t=PACK))
         n1_t = load_list("n1_t", n1)
         n2_t = load_list("n2_t", n2)
         w2_raw = sb("w2_raw", [P, PACK, N], F32)
@@ -141,19 +141,20 @@ def tile_picked_cdjoinclampbminmx_none_p_kernel(
 
         y_n1 = sb("y_n1", [P, TILES, S], F32)
         y_n2 = sb("y_n2", [P, TILES, S], F32)
-        larger = sb("larger", [P, TILES, S], F32)
         for t in range(TILES):
             nc.scalar.activation(y_win[t][:, :S], y_bank[t][:], ACT.Copy, scale=gain_abs[:, t : t + 1])
         for t in range(TILES):
             gather_on("scalar", y_n1[:, t, :], y_win[t], n1_t)
-            gather_on("vector", y_n2[:, t, :], y_win[t], n2_t)
-            nc.vector.scalar_tensor_tensor(
-                larger[:, t, :], y_bank[t][:], gain_abs[:, t : t + 1], y_n1[:, t, :], ALU.mult, ALU.max
-            )
+            gather_on("vector" if t < TILES - 1 else "scalar", y_n2[:, t, :], y_win[t], n2_t)
         dw_k1 = gather_v("dw_k1", dw, k1_t, U32)
         b_bank = [psum.tile([P, S], F32, name=f"b_bank{t}", tag=f"b{t}") for t in range(TILES)]
         for t in range(TILES):
             product(b_bank[t], (dw_k1, ds_placed), (xw_two, xs_two), t)
+        larger = sb("larger", [P, TILES, S], F32, tag="dw")
+        for t in range(TILES):
+            nc.vector.scalar_tensor_tensor(
+                larger[:, t, :], y_bank[t][:], gain_abs[:, t : t + 1], y_n1[:, t, :], ALU.mult, ALU.max
+            )
         w2q = quantize("w2q", w2_grouped[:].rearrange("p c j -> p (c j)"))
         z_grouped = sb("z_grouped", [P, S, PACK], BF16, tag="w2_grouped")
         z_codes = sb("z_codes", [P, S], U32)
@@ -179,7 +180,7 @@ def tile_picked_cdjoinclampbminmx_none_p_kernel(
         for t in range(TILES):
             nc.scalar.activation(b_win[t][:, :S], b_bank[t][:], ACT.Copy, scale=0.0625)
         last = TILES - 1
-        b_n5_early = sb("b_n5_early", [P, last, S], F32, tag="larger")
+        b_n5_early = sb("b_n5_early", [P, last, S], F32, tag="dw")
         b_n4 = [sb(f"b_n4_{t}", [P, S], F32)[:] for t in range(last)]
         b_n5 = [b_n5_early[:, t, :] for t in range(last)]
         for t in range(last):

from contextlib import ExitStack

import concourse.mybir as mybir

K, T, S, N, H, G = 512, 2048, 512, 512, 512, 2048
FLOPS = 2 * (K * H * S + H * N * S + K * H * S)

F32 = mybir.dt.float32
BF16 = mybir.dt.bfloat16
I32 = mybir.dt.int32
U32 = mybir.dt.uint32
U16 = mybir.dt.uint16
U8 = mybir.dt.uint8
FP8X4 = mybir.dt.float8_e4m3fn_x4
ALU = mybir.AluOpType
ACT = mybir.ActivationFunctionType

P = 128
PACK = 4
TILES = 4
Y_WINDOW = 1024
AB_WINDOW = 704


def tile_picked_cdjoinclampbminmx_none_p_kernel(
    tc, x_words, x_scales, w1, gn, w2, d_words, d_scales, offs, n1, n2, two, k1, n3, n4, n5, out
):
    nc = tc.nc
    with ExitStack() as ctx:
        keep = ctx.enter_context(tc.tile_pool(name="keep", bufs=1))
        psum = ctx.enter_context(tc.psum_pool(name="psum", bufs=1))

        def sb(name, shape, dtype, tag=None):
            return keep.tile(shape, dtype, name=name, tag=tag or name, align_bytes=64)

        def load_list(name, dram):
            tile = sb(name, [P, S // 16], U16)
            nc.sync.dma_start(tile[:], dram)
            return tile

        def load_words(name, dram):
            tile = sb(name, [P, T], U32)
            nc.sync.dma_start(tile[:].bitcast(I32), dram[0].rearrange("p n t -> p (n t)").bitcast(I32))
            return tile

        def zeroed_bytes(name, width, engine):
            tile = sb(name, [P, width], U8)
            engine.memset(tile[:].bitcast(I32), 0)
            return tile

        def gather_v(name, window, lst, dtype):
            tile = sb(name, [P, S], dtype)
            nc.vector.tensor_copy(tile[:], window[:].indirect(lst[:]))
            return tile

        def gather_on(engine, dst, window, lst):
            if engine == "vector":
                nc.vector.tensor_copy(dst, window[:].indirect(lst[:]))
            else:
                nc.scalar.activation(dst, window[:].indirect(lst[:]), ACT.Copy)

        def quantize(name, grouped):
            codes = sb(name + "_codes", [P, S], U32)
            scales = sb(name + "_scales", [P, S], U8)
            nc.vector.quantize_mx(out=codes[:].bitcast(FP8X4), scales=scales[:], in_=grouped)
            return codes, scales

        def product(bank, lhs, rhs, t):
            cols = slice(P * t, P * (t + 1))
            nc.tensor.matmul_mx(
                out=bank[:], lhsT=lhs[0][:, cols].bitcast(FP8X4), lhsT_scale=lhs[1][:, cols],
                rhs=rhs[0][:].bitcast(FP8X4), rhs_scale=rhs[1][:], start=True, stop=True,
            )

        xs = zeroed_bytes("xs", T, nc.vector)
        ds = zeroed_bytes("ds", G, nc.vector)
        ds_placed = zeroed_bytes("ds_placed", S, nc.vector)
        w1_rows = w1.rearrange("(p j) c -> p j c", j=PACK)
        w1_half = [sb(f"w1_half{h}", [P, PACK, H // 2], F32) for h in range(2)]

        offs_t = load_list("offs_t", offs)
        k1_t = load_list("k1_t", k1)
        nc.sync.dma_start(w1_half[0][:], w1_rows[:, :, : H // 2])
        for q in range(4):
            nc.sync.dma_start(xs[32 * q : 32 * q + 4, :].bitcast(I32), x_scales[0, 4 * q : 4 * q + 4, :].bitcast(I32))
        nc.sync.dma_start(w1_half[1][:], w1_rows[:, :, H // 2 :])
        nc.sync.dma_start(ds[0:P:8, :].bitcast(I32), d_scales[0].bitcast(I32))
        xw = load_words("xw", x_words)
        two_t = load_list("two_t", two)
        gain = sb("gain", [P, PACK], F32)
        nc.gpsimd.dma_start(gain[:], gn.rearrange("(p t) o -> p (t o)", t=PACK))
        n1_t = load_list("n1_t", n1)
        n2_t = load_list("n2_t", n2)
        w2_raw = sb("w2_raw", [P, PACK, N], F32)
        nc.sync.dma_start(w2_raw[:], w2.rearrange("(p j) c -> p j c", j=PACK))
        dw = load_words("dw", d_words)
        n4_t = load_list("n4_t", n4)
        n5_t = load_list("n5_t", n5)
        n3_t = load_list("n3_t", n3)

        y_win = [sb(f"y_win{t}", [P, Y_WINDOW], F32) for t in range(TILES)]
        a_win = [sb(f"a_win{t}", [P, AB_WINDOW], F32) for t in range(TILES)]
        b_win = [sb(f"b_win{t}", [P, AB_WINDOW], F32) for t in range(TILES)]
        for t in range(TILES):
            nc.vector.memset(y_win[t][:, S:], 0.0)
        for t in range(TILES):
            nc.gpsimd.memset(b_win[t][:, S:], 0.0)
            nc.gpsimd.memset(a_win[t][:, S:], 0.0)

        w1_grouped = sb("w1_grouped", [P, TILES, P, PACK], BF16)
        for h in range(2):
            nc.scalar.copy(
                w1_grouped[:, :, 64 * h : 64 * (h + 1), :].rearrange("p t m j -> p m j t"),
                w1_half[h][:].rearrange("p j (m t) -> p m j t", t=TILES),
            )
        gain_abs = sb("gain_abs", [P, PACK], F32)
        gain_sign = sb("gain_sign", [P, PACK], F32)
        nc.scalar.activation(gain_abs[:], gain[:], ACT.Abs)
        nc.scalar.activation(gain_sign[:], gain[:], ACT.Sign)

        xs_offs = gather_v("xs_offs", xs, offs_t, U8)
        w1q = quantize("w1q", w1_grouped[:].rearrange("p t m j -> p (t m j)"))
        xw_offs = gather_v("xw_offs", xw, offs_t, U32)
        y_bank = [psum.tile([P, S], F32, name=f"y_bank{t}", tag=f"ya{t}") for t in range(TILES)]
        for t in range(TILES):
            product(y_bank[t], w1q, (xw_offs, xs_offs), t)

        xs_two = gather_v("xs_two", xs, two_t, U8)
        ds_k1 = gather_v("ds_k1", ds, k1_t, U8)
        for q in range(4):
            nc.sync.dma_start(ds_placed[32 * q : 32 * q + 4, :].bitcast(I32), ds_k1[32 * q : 32 * q + 32 : 8, :].bitcast(I32))
        xw_two = gather_v("xw_two", xw, two_t, U32)

        w2_grouped = sb("w2_grouped", [P, N, PACK], BF16)
        nc.gpsimd.tensor_tensor(
            w2_grouped[:].rearrange("p (c i) j -> p c j i", i=4),
            w2_raw[:].rearrange("p j (c i) -> p c j i", i=4),
            gain_sign[:].unsqueeze(1).unsqueeze(3).to_broadcast([P, N // 4, PACK, 4]),
            ALU.mult,
        )

        y_n1 = sb("y_n1", [P, TILES, S], F32)
        y_n2 = sb("y_n2", [P, TILES, S], F32)
        for t in range(TILES):
            nc.scalar.activation(y_win[t][:, :S], y_bank[t][:], ACT.Copy, scale=gain_abs[:, t : t + 1])
        for t in range(TILES):
            gather_on("scalar", y_n1[:, t, :], y_win[t], n1_t)
            gather_on("vector" if t < TILES - 1 else "scalar", y_n2[:, t, :], y_win[t], n2_t)
        dw_k1 = gather_v("dw_k1", dw, k1_t, U32)
        b_bank = [psum.tile([P, S], F32, name=f"b_bank{t}", tag=f"b{t}") for t in range(TILES)]
        for t in range(TILES):
            product(b_bank[t], (dw_k1, ds_placed), (xw_two, xs_two), t)
        larger = sb("larger", [P, TILES, S], F32, tag="dw")
        for t in range(TILES):
            nc.vector.scalar_tensor_tensor(
                larger[:, t, :], y_bank[t][:], gain_abs[:, t : t + 1], y_n1[:, t, :], ALU.mult, ALU.max
            )
        w2q = quantize("w2q", w2_grouped[:].rearrange("p c j -> p (c j)"))
        z_grouped = sb("z_grouped", [P, S, PACK], BF16, tag="w2_grouped")
        z_codes = sb("z_codes", [P, S], U32)
        z_scales = sb("z_scales", [P, S], U8)
        for h in range(2):
            cols = slice(256 * h, 256 * (h + 1))
            nc.vector.tensor_tensor(
                z_grouped[:, cols, :].rearrange("p (c i) t -> p c t i", i=4),
                larger[:, :, cols].rearrange("p t (c i) -> p c t i", i=4),
                y_n2[:, :, cols].rearrange("p t (c i) -> p c t i", i=4),
                ALU.min,
            )
        for h in range(2):
            cols = slice(256 * h, 256 * (h + 1))
            nc.vector.quantize_mx(
                out=z_codes[:, cols].bitcast(FP8X4), scales=z_scales[:, cols],
                in_=z_grouped[:, cols, :].rearrange("p c t -> p (c t)"),
            )
        a_bank = [psum.tile([P, S], F32, name=f"a_bank{t}", tag=f"ya{t}") for t in range(TILES)]
        for t in range(TILES):
            product(a_bank[t], w2q, (z_codes, z_scales), t)

        for t in range(TILES):
            nc.scalar.activation(b_win[t][:, :S], b_bank[t][:], ACT.Copy, scale=0.0625)
        last = TILES - 1
        b_n5_early = sb("b_n5_early", [P, last, S], F32, tag="dw")
        b_n4 = [sb(f"b_n4_{t}", [P, S], F32)[:] for t in range(last)]
        b_n5 = [b_n5_early[:, t, :] for t in range(last)]
        for t in range(last):
            gather_on("scalar", b_n4[t], b_win[t], n4_t)
            gather_on("vector", b_n5[t], b_win[t], n5_t)
        for t in range(TILES):
            a_n3 = sb(f"a_n3_{t}", [P, S], F32)
            nc.scalar.copy(a_win[t][:, :S], a_bank[t][:])
            gather_on("scalar", a_n3[:], a_win[t], n3_t)
            if t == last:
                b_n4.append(sb("b_n4_last", [P, S], F32, tag=f"a_win{t - 1}")[:])
                b_n5.append(sb("b_n5_last", [P, S], F32, tag=f"a_win{t}")[:])
                gather_on("scalar", b_n4[t], b_win[t], n4_t)
                gather_on("scalar", b_n5[t], b_win[t], n5_t)
            diff = sb(f"diff{t}", [P, S], F32)
            low = sb(f"low{t}", [P, S], F32)
            res = sb(f"res{t}", [P, S], F32)
            nc.vector.scalar_tensor_tensor(diff[:], a_n3[:], -0.5, a_bank[t][:], ALU.mult, ALU.add)
            nc.vector.tensor_tensor(low[:], diff[:], b_n4[t], ALU.min)
            nc.vector.tensor_tensor(res[:], low[:], b_n5[t], ALU.max)
            nc.sync.dma_start(out[P * t : P * (t + 1), :], res[:])
